import numpy as np
import ml_dtypes


def mxq(x, axis, fmt="e4m3"):
    dtype, down = {"e4m3": (ml_dtypes.float8_e4m3fn, 7), "e5m2": (ml_dtypes.float8_e5m2, 14)}[fmt]
    v = np.moveaxis(np.asarray(x, np.float32).astype(ml_dtypes.bfloat16).astype(np.float64), axis, -1)
    blocks = v.reshape(v.shape[:-1] + (-1, 32))
    amax = np.abs(blocks).max(-1, keepdims=True)
    byte = np.maximum(np.where(amax > 0, np.frexp(amax)[1] - 1 + 127, 0) - down, 1)
    scale = np.exp2(byte - 127.0)
    codes = (blocks / scale).astype(np.float32).astype(dtype).astype(np.float64)
    return np.moveaxis((codes * scale).reshape(v.shape), -1, axis)


WIDE = False


def mx_kscale(k):
    if not WIDE:
        return np.ones(k)
    levels = np.array([30, -30])
    if k % 512:
        return np.exp2(np.random.permutation(np.resize(levels, k // 32))).repeat(32)
    a = np.empty((k // 512, 16))
    for p in range(k // 512):
        a[p, :8] = np.random.permutation(np.resize(levels, 8))
        for g in range(8):
            far = levels[np.abs(levels - a[p, g]) >= 10]
            a[p, g + 8] = far[np.random.randint(len(far))]
    return np.exp2(a.ravel()).repeat(32)


def f64(x):
    return np.asarray(x).astype(np.float64)


def striped(idx):
    return np.tile(np.asarray(idx).reshape(-1, 16).T, (8, 1)).astype(np.uint16)


def unstriped(offs):
    return offs[:16].T.reshape(-1).astype(np.int64)


E2M1 = np.array([0.0, 0.5, 1.0, 1.5, 2.0, 3.0, 4.0, 6.0, -0.0, -0.5, -1.0, -1.5, -2.0, -3.0, -4.0, -6.0])


def pack_weight(w, fmt):
    k, n = w.shape
    w = f64(np.asarray(w, np.float32).astype(ml_dtypes.bfloat16)).reshape(k // 32, 32, n)
    amax = np.abs(w).max(1)
    if fmt in ("e4m3", "e5m2"):
        byte = np.frexp(amax)[1] - 1 + 127 - (7 if fmt == "e4m3" else 14)
    else:
        mant, ex = np.frexp(amax / 6.0)
        byte = np.where(mant > 0.5, ex, ex - 1) + 127
    byte = np.clip(np.where(amax > 0, byte, 1), 1, 254)
    scaled = (w * np.exp2(127.0 - byte)[:, None, :]).reshape(k, n).astype(np.float32)
    by_word = np.ascontiguousarray(scaled.reshape(k // 512, 128, 4, n).transpose(0, 1, 3, 2))
    if fmt in ("e4m3", "e5m2"):
        words = by_word.astype(ml_dtypes.float8_e4m3fn if fmt == "e4m3" else ml_dtypes.float8_e5m2).view(np.uint8)
    else:
        c = by_word.astype(ml_dtypes.float4_e2m1fn).view(np.uint8) & 0xF
        words = (c[..., 0::2] | (c[..., 1::2] << 4)).reshape(k // 512, 128, 2 * n)
    return np.ascontiguousarray(words), np.ascontiguousarray(byte.astype(np.uint8).reshape(k // 512, 16, n))


def unpack_weight(words, scales, fmt):
    g, _, n = scales.shape
    words = np.ascontiguousarray(words).reshape(g, 128, n, -1)
    if fmt in ("e4m3", "e5m2"):
        vals = words.view(ml_dtypes.float8_e4m3fn if fmt == "e4m3" else ml_dtypes.float8_e5m2).astype(np.float64)
    else:
        nib = np.empty((g, 128, n, 4), np.uint8)
        nib[..., 0::2] = words & 0xF
        nib[..., 1::2] = words >> 4
        vals = E2M1[nib]
    vals = vals * np.repeat(np.exp2(scales.astype(np.float64) - 127.0), 8, axis=1)[..., None]
    return vals.transpose(0, 1, 3, 2).reshape(g * 512, n)


def sigmoid(v):
    return 1.0 / (1.0 + np.exp(-v))


K, T, Z, J, R, Q, N, E = 512, 1024, 1024, 256, 512, 1024, 256, 1024


def setup_inputs():
    n = np.random.standard_normal
    idx = np.random.permutation(T)[:J]
    idx2 = np.random.permutation(Z)[:J]
    idx3 = np.random.permutation(Q)[:J]
    idx4 = np.random.permutation(E)[:J]
    fk = mx_kscale(K)
    fr = mx_kscale(R)
    xtp = pack_weight(n((K, T)) / fk[:, None], "e2m1")
    xop = pack_weight(n((K, Z)) / fk[:, None], "e4m3")
    wp = pack_weight(n((K, R)) * 1 / np.sqrt(K) * fk[:, None] * fr, "e4m3")
    w2p = pack_weight(n((K, R)) * 1 / np.sqrt(K) * fk[:, None] * fr, "e5m2")
    wbp = pack_weight(n((R, N)) * 1 / np.sqrt(R) / fr[:, None], "e2m1")
    return {
        "xt_words": xtp[0],
        "xt_scales": xtp[1],
        "xo_words": xop[0],
        "xo_scales": xop[1],
        "w_words": wp[0],
        "w_scales": wp[1],
        "w2_words": w2p[0],
        "w2_scales": w2p[1],
        "tg": (1.0 * n((R, Q))).astype(np.float32),
        "sg": (np.random.uniform(0.6, 1.6, (R, 1))).astype(np.float32),
        "bg": (np.random.uniform(-1.0, 1.0, (R, 1))).astype(np.float32),
        "wb_words": wbp[0],
        "wb_scales": wbp[1],
        "tz": (n((N, E))).astype(np.float32),
        "offs": striped(idx),
        "offs2": striped(idx2),
        "offs3": striped(idx3),
        "offs4": striped(idx4),
    }


def reference(xt_words, xt_scales, xo_words, xo_scales, w_words, w_scales, w2_words, w2_scales, tg, sg, bg, wb_words, wb_scales, tz, offs, offs2, offs3, offs4):
    idx = unstriped(offs)
    idx2 = unstriped(offs2)
    idx3 = unstriped(offs3)
    idx4 = unstriped(offs4)
    xtu = unpack_weight(xt_words, xt_scales, "e2m1")
    xou = unpack_weight(xo_words, xo_scales, "e4m3")
    wu = unpack_weight(w_words, w_scales, "e4m3")
    w2u = unpack_weight(w2_words, w2_scales, "e5m2")
    wbu = unpack_weight(wb_words, wb_scales, "e2m1")
    xtidxg = xtu[:, idx]
    xoidx2g = xou[:, idx2]
    a = wu.T @ xtidxg + w2u.T @ xoidx2g
    b = w2u.T @ xtidxg + wu.T @ xoidx2g
    hid = np.maximum(a, b) * sigmoid(f64(tg)[:, idx3] * f64(sg) + f64(bg))
    hidq = mxq(hid, 0, "e5m2")
    p = wbu.T @ hidq
    y = p + f64(tz)[:, idx4]
    return y

@@ -1,0 +1,184 @@
+from contextlib import ExitStack
+
+import concourse.mybir as mybir
+
+K, T, Z, J, R, Q, N, E = 512, 1024, 1024, 256, 512, 1024, 256, 1024
+FLOPS = 2 * K * R * J * 4 + 2 * R * N * J
+
+F32 = mybir.dt.float32
+BF16 = mybir.dt.bfloat16
+I32 = mybir.dt.int32
+U32 = mybir.dt.uint32
+U16 = mybir.dt.uint16
+U8 = mybir.dt.uint8
+E4M3 = mybir.dt.float8_e4m3fn_x4
+E5M2 = mybir.dt.float8_e5m2_x4
+E2M1 = mybir.dt.float4_e2m1fn_x4
+ACT = mybir.ActivationFunctionType
+ALU = mybir.AluOpType
+
+P = 128
+PACK = 4
+
+
+def load_scale_rows(queue, plane, scales):
+    rows = scales[0].bitcast(I32)
+    for quad in range(4):
+        queue.dma_start(out=plane[32 * quad : 32 * quad + 4, :].bitcast(I32), in_=rows[4 * quad : 4 * quad + 4, :])
+
+
+def tile_list_crossed_tablegate_one_tabled_kernel(
+    tc, xt_words, xt_scales, xo_words, xo_scales, w_words, w_scales, w2_words, w2_scales,
+    tg, sg, bg, wb_words, wb_scales, tz, offs, offs2, offs3, offs4, out,
+):
+    nc = tc.nc
+    with ExitStack() as ctx:
+        sb = ctx.enter_context(tc.tile_pool(name="sb", bufs=1))
+        ps = ctx.enter_context(tc.psum_pool(name="ps", bufs=1))
+
+        list_xt = sb.tile([P, J // 16], U16, name="list_xt")
+        list_xo = sb.tile([P, J // 16], U16, name="list_xo")
+        list_tg = sb.tile([P, J // 16], U16, name="list_tg")
+        list_tz = sb.tile([P, J // 16], U16, name="list_tz")
+        xt_w = sb.tile([P, T], U16, name="xt_w", align_bytes=64)
+        xt_s = sb.tile([P, T], U8, name="xt_s", align_bytes=64)
+        xo_w = sb.tile([P, Z], U32, name="xo_w", align_bytes=64)
+        xo_s = sb.tile([P, Z], U8, name="xo_s", align_bytes=64)
+        w_w = sb.tile([P, R], U32, name="w_w", align_bytes=64)
+        w_s = sb.tile([P, R], U8, name="w_s", align_bytes=64)
+        w2_w = sb.tile([P, R], U32, name="w2_w", align_bytes=64)
+        w2_s = sb.tile([P, R], U8, name="w2_s", align_bytes=64)
+        wb_w = sb.tile([P, 2 * N], U8, name="wb_w", align_bytes=64)
+        wb_s = sb.tile([P, N], U8, name="wb_s", align_bytes=64)
+        slope = sb.tile([P, PACK], F32, name="slope")
+        offset = sb.tile([P, PACK], F32, name="offset")
+        tg_rows = [sb.tile([P, Q], F32, name=f"tg_rows{t}") for t in range(PACK)]
+        tz_rows = [sb.tile([P, E], F32, name=f"tz_rows{h}") for h in range(2)]
+
+        nc.vector.memset(xt_s[:].bitcast(I32), 0)
+        nc.vector.memset(w_s[:].bitcast(I32), 0)
+        nc.vector.memset(w2_s[:].bitcast(I32), 0)
+        nc.gpsimd.memset(xo_s[:].bitcast(I32), 0)
+        nc.vector.memset(wb_s[:].bitcast(I32), 0)
+
+        tg_by_slot = tg.rearrange("(p t) q -> t p q", t=PACK)
+
+        nc.sync.dma_start(out=xt_w[:].bitcast(I32), in_=xt_words[0].bitcast(I32))
+        nc.sync.dma_start(out=xo_w[:].bitcast(I32), in_=xo_words[0].rearrange("p c r -> p (c r)").bitcast(I32))
+        nc.sync.dma_start(list_xt[:], offs)
+        load_scale_rows(nc.sync, xt_s, xt_scales)
+        nc.sync.dma_start(out=w_w[:].bitcast(I32), in_=w_words[0].rearrange("p c r -> p (c r)").bitcast(I32))
+        nc.sync.dma_start(out=tg_rows[0][:], in_=tg_by_slot[0])
+        load_scale_rows(nc.sync, w_s, w_scales)
+        nc.sync.dma_start(list_xo[:], offs2)
+        nc.sync.dma_start(out=w2_w[:].bitcast(I32), in_=w2_words[0].rearrange("p c r -> p (c r)").bitcast(I32))
+        nc.sync.dma_start(out=tg_rows[1][:], in_=tg_by_slot[1])
+        load_scale_rows(nc.sync, w2_s, w2_scales)
+        nc.sync.dma_start(out=tg_rows[2][:], in_=tg_by_slot[2])
+        nc.sync.dma_start(list_tg[:], offs3)
+        nc.sync.dma_start(out=tg_rows[3][:], in_=tg_by_slot[3])
+        load_scale_rows(nc.sync, wb_s, wb_scales)
+        nc.sync.dma_start(out=tz_rows[0][:], in_=tz[0:P, :])
+        nc.sync.dma_start(list_tz[:], offs4)
+        nc.sync.dma_start(out=wb_w[:].bitcast(I32), in_=wb_words[0].bitcast(I32))
+        nc.sync.dma_start(out=tz_rows[1][:], in_=tz[P : 2 * P, :])
+
+        load_scale_rows(nc.gpsimd, xo_s, xo_scales)
+        nc.gpsimd.dma_start(out=slope[:], in_=sg.rearrange("(p t) o -> p (t o)", t=PACK))
+        nc.gpsimd.dma_start(out=offset[:], in_=bg.rearrange("(p t) o -> p (t o)", t=PACK))
+
+        xt_gw = sb.tile([P, J], U16, name="xt_gw", align_bytes=64)
+        xt_gs = sb.tile([P, J], U8, name="xt_gs", align_bytes=64)
+        xo_gw = sb.tile([P, J], U32, name="xo_gw", align_bytes=64)
+        xo_gs = sb.tile([P, J], U8, name="xo_gs", align_bytes=64)
+        w_dw = sb.tile([P, R], U32, name="w_dw", align_bytes=64)
+        w_ds = sb.tile([P, R], U8, name="w_ds", align_bytes=64)
+        w2_dw = sb.tile([P, R], U32, name="w2_dw", align_bytes=64)
+        w2_ds = sb.tile([P, R], U8, name="w2_ds", align_bytes=64)
+
+        def deal_words(dst, src):
+            nc.vector.tensor_copy(
+                out=dst[:].bitcast(I32).rearrange("p (t c i) -> p c t i", t=PACK, i=4),
+                in_=src[:].bitcast(I32).rearrange("p (c i t) -> p c t i", t=PACK, i=4),
+            )
+
+        def deal_scales(dst, src):
+            nc.vector.tensor_copy(
+                out=dst[:].rearrange("p (t m) -> p t m", t=PACK),
+                in_=src[:].rearrange("p (m t) -> p t m", t=PACK),
+            )
+
+        nc.vector.tensor_copy(xt_gw[:], xt_w[:].indirect(list_xt[:]))
+        nc.vector.tensor_copy(xt_gs[:], xt_s[:].indirect(list_xt[:]))
+        deal_words(w_dw, w_w)
+        deal_scales(w_ds, w_s)
+        nc.vector.tensor_copy(xo_gw[:], xo_w[:].indirect(list_xo[:]))
+        nc.vector.tensor_copy(xo_gs[:], xo_s[:].indirect(list_xo[:]))
+        deal_words(w2_dw, w2_w)
+        deal_scales(w2_ds, w2_s)
+
+        a_bank = [ps.tile([P, 2, J], F32, name=f"a_bank{u}") for u in range(2)]
+        b_bank = [ps.tile([P, 2, J], F32, name=f"b_bank{u}") for u in range(2)]
+        first = (w_dw, w_ds, E4M3)
+        second = (w2_dw, w2_ds, E5M2)
+        tokens = (xt_gw, xt_gs, E2M1)
+        notes = (xo_gw, xo_gs, E4M3)
+
+        def product(bank, u, weight, moving, opens):
+            for i in range(2):
+                cols = slice((2 * u + i) * P, (2 * u + i + 1) * P)
+                nc.tensor.matmul_mx(
+                    out=bank[u][:, i, :],
+                    lhsT=weight[0][:, cols].bitcast(weight[2]),
+                    lhsT_scale=weight[1][:, cols],
+                    rhs=moving[0][:].bitcast(moving[2]),
+                    rhs_scale=moving[1][:],
+                    start=(opens and i == 0),
+                    stop=(not opens and i == 1),
+                )
+
+        for u in range(2):
+            product(a_bank, u, first, tokens, True)
+        for u in range(2):
+            product(b_bank, u, first, notes, True)
+        for u in range(2):
+            product(a_bank, u, second, notes, False)
+            product(b_bank, u, second, tokens, False)
+
+        gate = sb.tile([P, PACK, J], F32, name="gate")
+        hid = sb.tile([P, J, PACK], BF16, name="hid", align_bytes=64)
+        for u in range(2):
+            for t in range(2 * u, 2 * u + 2):
+                nc.scalar.activation(
+                    out=gate[:, t, :], in_=tg_rows[t][:].indirect(list_tg[:]), func=ACT.Sigmoid,
+                    bias=offset[:, t : t + 1], scale=slope[:, t : t + 1],
+                )
+            a_sb = sb.tile([P, J, 2], F32, name=f"a_sb{u}")
+            nc.scalar.copy(out=a_sb[:], in_=a_bank[u][:].rearrange("p i j -> p j i"))
+            larger = sb.tile([P, J, 2], F32, name=f"larger{u}")
+            nc.vector.tensor_tensor(larger[:], b_bank[u][:].rearrange("p i j -> p j i"), a_sb[:], ALU.max)
+            nc.vector.tensor_tensor(
+                hid[:, :, 2 * u : 2 * u + 2], larger[:],
+                gate[:, 2 * u : 2 * u + 2, :].rearrange("p i j -> p j i"), ALU.mult,
+            )
+
+        hid_w = sb.tile([P, J], U32, name="hid_w", align_bytes=64)
+        hid_s = sb.tile([P, J], U8, name="hid_s", align_bytes=64)
+        nc.vector.quantize_mx(out=hid_w[:].bitcast(E5M2), scales=hid_s[:], in_=hid[:].rearrange("p j t -> p (j t)"))
+
+        for h in range(2):
+            picked = sb.tile([P, J], F32, name=f"picked{h}")
+            nc.scalar.activation(out=picked[:], in_=tz_rows[h][:].indirect(list_tz[:]), func=ACT.Copy)
+            p_bank = ps.tile([P, J], F32, name=f"p_bank{h}")
+            nc.tensor.matmul_mx(
+                out=p_bank[:],
+                lhsT=wb_w[:, 2 * h * P : 2 * (h + 1) * P].bitcast(E2M1),
+                lhsT_scale=wb_s[:, h * P : (h + 1) * P],
+                rhs=hid_w[:].bitcast(E5M2),
+                rhs_scale=hid_s[:],
+                start=True,
+                stop=True,
+            )
+            result = sb.tile([P, J], F32, name=f"result{h}")
+            nc.vector.tensor_tensor(result[:], p_bank[:], picked[:], ALU.add)
+            nc.sync.dma_start(out=out[h * P : (h + 1) * P, :], in_=result[:])

@@ -21,9 +21,9 @@ P = 128
 PACK = 4
 
 
-def load_scale_rows(queue, plane, scales):
+def load_scale_rows(queue, plane, scales, quads=(0, 1, 2, 3)):
     rows = scales[0].bitcast(I32)
-    for quad in range(4):
+    for quad in quads:
         queue.dma_start(out=plane[32 * quad : 32 * quad + 4, :].bitcast(I32), in_=rows[4 * quad : 4 * quad + 4, :])
 
 
@@ -57,35 +57,36 @@ def tile_list_crossed_tablegate_one_tabled_kernel(
 
         nc.vector.memset(xt_s[:].bitcast(I32), 0)
         nc.vector.memset(w_s[:].bitcast(I32), 0)
+        nc.vector.memset(xo_s[:].bitcast(I32), 0)
         nc.vector.memset(w2_s[:].bitcast(I32), 0)
-        nc.gpsimd.memset(xo_s[:].bitcast(I32), 0)
         nc.vector.memset(wb_s[:].bitcast(I32), 0)
 
         tg_by_slot = tg.rearrange("(p t) q -> t p q", t=PACK)
 
         nc.sync.dma_start(out=xt_w[:].bitcast(I32), in_=xt_words[0].bitcast(I32))
-        nc.sync.dma_start(out=xo_w[:].bitcast(I32), in_=xo_words[0].rearrange("p c r -> p (c r)").bitcast(I32))
         nc.sync.dma_start(list_xt[:], offs)
         load_scale_rows(nc.sync, xt_s, xt_scales)
         nc.sync.dma_start(out=w_w[:].bitcast(I32), in_=w_words[0].rearrange("p c r -> p (c r)").bitcast(I32))
-        nc.sync.dma_start(out=tg_rows[0][:], in_=tg_by_slot[0])
+        nc.sync.dma_start(out=xo_w[:].bitcast(I32), in_=xo_words[0].rearrange("p c r -> p (c r)").bitcast(I32))
         load_scale_rows(nc.sync, w_s, w_scales)
         nc.sync.dma_start(list_xo[:], offs2)
         nc.sync.dma_start(out=w2_w[:].bitcast(I32), in_=w2_words[0].rearrange("p c r -> p (c r)").bitcast(I32))
-        nc.sync.dma_start(out=tg_rows[1][:], in_=tg_by_slot[1])
+        nc.sync.dma_start(list_tg[:], offs3)
+        load_scale_rows(nc.sync, xo_s, xo_scales)
         load_scale_rows(nc.sync, w2_s, w2_scales)
         nc.sync.dma_start(out=tg_rows[2][:], in_=tg_by_slot[2])
-        nc.sync.dma_start(list_tg[:], offs3)
         nc.sync.dma_start(out=tg_rows[3][:], in_=tg_by_slot[3])
-        load_scale_rows(nc.sync, wb_s, wb_scales)
         nc.sync.dma_start(out=tz_rows[0][:], in_=tz[0:P, :])
         nc.sync.dma_start(list_tz[:], offs4)
         nc.sync.dma_start(out=wb_w[:].bitcast(I32), in_=wb_words[0].bitcast(I32))
+        load_scale_rows(nc.sync, wb_s, wb_scales, (0, 1))
         nc.sync.dma_start(out=tz_rows[1][:], in_=tz[P : 2 * P, :])
 
-        load_scale_rows(nc.gpsimd, xo_s, xo_scales)
-        nc.gpsimd.dma_start(out=slope[:], in_=sg.rearrange("(p t) o -> p (t o)", t=PACK))
         nc.gpsimd.dma_start(out=offset[:], in_=bg.rearrange("(p t) o -> p (t o)", t=PACK))
+        nc.gpsimd.dma_start(out=slope[:], in_=sg.rearrange("(p t) o -> p (t o)", t=PACK))
+        nc.gpsimd.dma_start(out=tg_rows[0][:], in_=tg_by_slot[0])
+        nc.gpsimd.dma_start(out=tg_rows[1][:], in_=tg_by_slot[1])
+        load_scale_rows(nc.gpsimd, wb_s, wb_scales, (2, 3))
 
         xt_gw = sb.tile([P, J], U16, name="xt_gw", align_bytes=64)
         xt_gs = sb.tile([P, J], U8, name="xt_gs", align_bytes=64)
@@ -102,10 +103,10 @@ def tile_list_crossed_tablegate_one_tabled_kernel(
                 in_=src[:].bitcast(I32).rearrange("p (c i t) -> p c t i", t=PACK, i=4),
             )
 
-        def deal_scales(dst, src):
+        def deal_scales(dst, src, slots=slice(0, PACK)):
             nc.vector.tensor_copy(
-                out=dst[:].rearrange("p (t m) -> p t m", t=PACK),
-                in_=src[:].rearrange("p (m t) -> p t m", t=PACK),
+                out=dst[:].rearrange("p (t m) -> p t m", t=PACK)[:, slots, :],
+                in_=src[:].rearrange("p (m t) -> p t m", t=PACK)[:, slots, :],
             )
 
         nc.vector.tensor_copy(xt_gw[:], xt_w[:].indirect(list_xt[:]))
@@ -115,70 +116,94 @@ def tile_list_crossed_tablegate_one_tabled_kernel(
         nc.vector.tensor_copy(xo_gw[:], xo_w[:].indirect(list_xo[:]))
         nc.vector.tensor_copy(xo_gs[:], xo_s[:].indirect(list_xo[:]))
         deal_words(w2_dw, w2_w)
-        deal_scales(w2_ds, w2_s)
+        deal_scales(w2_ds, w2_s, slice(0, 2))
+        deal_scales(w2_ds, w2_s, slice(2, PACK))
 
-        a_bank = [ps.tile([P, 2, J], F32, name=f"a_bank{u}") for u in range(2)]
-        b_bank = [ps.tile([P, 2, J], F32, name=f"b_bank{u}") for u in range(2)]
+        a_bank = [ps.tile([P, J], F32, name=f"a_bank{t}", tag=f"left{t}") for t in range(PACK)]
+        b_bank = [ps.tile([P, J], F32, name=f"b_bank{t}", tag=f"right{t}") for t in range(PACK)]
         first = (w_dw, w_ds, E4M3)
         second = (w2_dw, w2_ds, E5M2)
         tokens = (xt_gw, xt_gs, E2M1)
         notes = (xo_gw, xo_gs, E4M3)
 
-        def product(bank, u, weight, moving, opens):
-            for i in range(2):
-                cols = slice((2 * u + i) * P, (2 * u + i + 1) * P)
-                nc.tensor.matmul_mx(
-                    out=bank[u][:, i, :],
-                    lhsT=weight[0][:, cols].bitcast(weight[2]),
-                    lhsT_scale=weight[1][:, cols],
-                    rhs=moving[0][:].bitcast(moving[2]),
-                    rhs_scale=moving[1][:],
-                    start=(opens and i == 0),
-                    stop=(not opens and i == 1),
-                )
+        def product(bank, t, weight, moving, opens):
+            cols = slice(t * P, (t + 1) * P)
+            nc.tensor.matmul_mx(
+                out=bank[t][:],
+                lhsT=weight[0][:, cols].bitcast(weight[2]),
+                lhsT_scale=weight[1][:, cols],
+                rhs=moving[0][:].bitcast(moving[2]),
+                rhs_scale=moving[1][:],
+                start=opens,
+                stop=not opens,
+            )
 
-        for u in range(2):
-            product(a_bank, u, first, tokens, True)
-        for u in range(2):
-            product(b_bank, u, first, notes, True)
-        for u in range(2):
-            product(a_bank, u, second, notes, False)
-            product(b_bank, u, second, tokens, False)
+        for t in range(PACK):
+            product(a_bank, t, first, tokens, True)
+        for t in range(PACK):
+            product(b_bank, t, first, notes, True)
+        for t in range(PACK):
+            product(a_bank, t, second, notes, False)
+            product(b_bank, t, second, tokens, False)
 
         gate = sb.tile([P, PACK, J], F32, name="gate")
         hid = sb.tile([P, J, PACK], BF16, name="hid", align_bytes=64)
-        for u in range(2):
-            for t in range(2 * u, 2 * u + 2):
-                nc.scalar.activation(
-                    out=gate[:, t, :], in_=tg_rows[t][:].indirect(list_tg[:]), func=ACT.Sigmoid,
-                    bias=offset[:, t : t + 1], scale=slope[:, t : t + 1],
-                )
-            a_sb = sb.tile([P, J, 2], F32, name=f"a_sb{u}")
-            nc.scalar.copy(out=a_sb[:], in_=a_bank[u][:].rearrange("p i j -> p j i"))
-            larger = sb.tile([P, J, 2], F32, name=f"larger{u}")
-            nc.vector.tensor_tensor(larger[:], b_bank[u][:].rearrange("p i j -> p j i"), a_sb[:], ALU.max)
-            nc.vector.tensor_tensor(
-                hid[:, :, 2 * u : 2 * u + 2], larger[:],
-                gate[:, 2 * u : 2 * u + 2, :].rearrange("p i j -> p j i"), ALU.mult,
+        a_sb = sb.tile([P, PACK, J], F32, name="a_sb")
+        larger = sb.tile([P, PACK, J], F32, name="larger")
+
+        def look_up_gate(t):
+            nc.scalar.activation(
+                out=gate[:, t, :], in_=tg_rows[t][:].indirect(list_tg[:]), func=ACT.Sigmoid,
+                bias=offset[:, t : t + 1], scale=slope[:, t : t + 1],
             )
+
+        def take_larger(t):
+            nc.vector.tensor_tensor(larger[:, t, :], b_bank[t][:], a_sb[:, t, :], ALU.max)
+
+        def gated(u, cols):
+            nc.vector.tensor_tensor(
+                hid[:, cols, 2 * u : 2 * u + 2],
+                larger[:, 2 * u : 2 * u + 2, cols].rearrange("p i j -> p j i"),
+                gate[:, 2 * u : 2 * u + 2, cols].rearrange("p i j -> p j i"), ALU.mult,
+            )
+
+        look_up_gate(0)
+        look_up_gate(1)
+        for t in range(PACK):
+            nc.scalar.copy(out=a_sb[:, t, :], in_=a_bank[t][:])
+        look_up_gate(2)
+        look_up_gate(3)
+        halves = [slice(0, J // 2), slice(J // 2, J)]
+        take_larger(0)
+        take_larger(1)
+        gated(0, slice(0, J))
+        take_larger(2)
+        take_larger(3)
+        for cols in halves:
+            gated(1, cols)
 
         hid_w = sb.tile([P, J], U32, name="hid_w", align_bytes=64)
         hid_s = sb.tile([P, J], U8, name="hid_s", align_bytes=64)
-        nc.vector.quantize_mx(out=hid_w[:].bitcast(E5M2), scales=hid_s[:], in_=hid[:].rearrange("p j t -> p (j t)"))
+        p_bank = [ps.tile([P, J], F32, name=f"p_bank{h}", tag=f"left{h}") for h in range(2)]
+        for cols in halves:
+            nc.vector.quantize_mx(
+                out=hid_w[:, cols].bitcast(E5M2), scales=hid_s[:, cols], in_=hid[:, cols, :].rearrange("p j t -> p (j t)")
+            )
+        for cols in halves:
+            for h in range(2):
+                nc.tensor.matmul_mx(
+                    out=p_bank[h][:, cols],
+                    lhsT=wb_w[:, 2 * h * P : 2 * (h + 1) * P].bitcast(E2M1),
+                    lhsT_scale=wb_s[:, h * P : (h + 1) * P],
+                    rhs=hid_w[:, cols].bitcast(E5M2),
+                    rhs_scale=hid_s[:, cols],
+                    start=True,
+                    stop=True,
+                )
 
         for h in range(2):
             picked = sb.tile([P, J], F32, name=f"picked{h}")
             nc.scalar.activation(out=picked[:], in_=tz_rows[h][:].indirect(list_tz[:]), func=ACT.Copy)
-            p_bank = ps.tile([P, J], F32, name=f"p_bank{h}")
-            nc.tensor.matmul_mx(
-                out=p_bank[:],
-                lhsT=wb_w[:, 2 * h * P : 2 * (h + 1) * P].bitcast(E2M1),
-                lhsT_scale=wb_s[:, h * P : (h + 1) * P],
-                rhs=hid_w[:].bitcast(E5M2),
-                rhs_scale=hid_s[:],
-                start=True,
-                stop=True,
-            )
             result = sb.tile([P, J], F32, name=f"result{h}")
-            nc.vector.tensor_tensor(result[:], p_bank[:], picked[:], ALU.add)
+            nc.vector.tensor_tensor(result[:], p_bank[h][:], picked[:], ALU.add)
             nc.sync.dma_start(out=out[h * P : (h + 1) * P, :], in_=result[:])

@@ -71,22 +71,22 @@ def tile_list_crossed_tablegate_one_tabled_kernel(
         load_scale_rows(nc.sync, w_s, w_scales)
         nc.sync.dma_start(list_xo[:], offs2)
         nc.sync.dma_start(out=w2_w[:].bitcast(I32), in_=w2_words[0].rearrange("p c r -> p (c r)").bitcast(I32))
+        nc.sync.dma_start(out=tg_rows[0][:], in_=tg_by_slot[0])
         nc.sync.dma_start(list_tg[:], offs3)
+        nc.sync.dma_start(out=tg_rows[1][:], in_=tg_by_slot[1])
         load_scale_rows(nc.sync, xo_s, xo_scales)
-        load_scale_rows(nc.sync, w2_s, w2_scales)
+        load_scale_rows(nc.sync, w2_s, w2_scales, (0, 1))
         nc.sync.dma_start(out=tg_rows[2][:], in_=tg_by_slot[2])
+        nc.sync.dma_start(list_tz[:], offs4)
         nc.sync.dma_start(out=tg_rows[3][:], in_=tg_by_slot[3])
         nc.sync.dma_start(out=tz_rows[0][:], in_=tz[0:P, :])
-        nc.sync.dma_start(list_tz[:], offs4)
         nc.sync.dma_start(out=wb_w[:].bitcast(I32), in_=wb_words[0].bitcast(I32))
-        load_scale_rows(nc.sync, wb_s, wb_scales, (0, 1))
+        load_scale_rows(nc.sync, wb_s, wb_scales)
         nc.sync.dma_start(out=tz_rows[1][:], in_=tz[P : 2 * P, :])
 
         nc.gpsimd.dma_start(out=offset[:], in_=bg.rearrange("(p t) o -> p (t o)", t=PACK))
         nc.gpsimd.dma_start(out=slope[:], in_=sg.rearrange("(p t) o -> p (t o)", t=PACK))
-        nc.gpsimd.dma_start(out=tg_rows[0][:], in_=tg_by_slot[0])
-        nc.gpsimd.dma_start(out=tg_rows[1][:], in_=tg_by_slot[1])
-        load_scale_rows(nc.gpsimd, wb_s, wb_scales, (2, 3))
+        load_scale_rows(nc.gpsimd, w2_s, w2_scales, (2, 3))
 
         xt_gw = sb.tile([P, J], U16, name="xt_gw", align_bytes=64)
         xt_gs = sb.tile([P, J], U8, name="xt_gs", align_bytes=64)
@@ -160,39 +160,47 @@ def tile_list_crossed_tablegate_one_tabled_kernel(
         def take_larger(t):
             nc.vector.tensor_tensor(larger[:, t, :], b_bank[t][:], a_sb[:, t, :], ALU.max)
 
-        def gated(u, cols):
-            nc.vector.tensor_tensor(
-                hid[:, cols, 2 * u : 2 * u + 2],
-                larger[:, 2 * u : 2 * u + 2, cols].rearrange("p i j -> p j i"),
-                gate[:, 2 * u : 2 * u + 2, cols].rearrange("p i j -> p j i"), ALU.mult,
-            )
+        def gated(t, cols):
+            nc.vector.tensor_tensor(hid_slots[:, t, cols], larger[:, t, cols], gate[:, t, cols], ALU.mult)
 
+        def free_a(t):
+            nc.scalar.copy(out=a_sb[:, t, :], in_=a_bank[t][:])
+
+        hid_slots = sb.tile([P, PACK, J], BF16, name="hid_slots")
+        halves = [slice(0, J // 2), slice(J // 2, J)]
         look_up_gate(0)
         look_up_gate(1)
-        for t in range(PACK):
-            nc.scalar.copy(out=a_sb[:, t, :], in_=a_bank[t][:])
+        free_a(0)
+        free_a(1)
         look_up_gate(2)
+        free_a(2)
+        free_a(3)
         look_up_gate(3)
-        halves = [slice(0, J // 2), slice(J // 2, J)]
-        take_larger(0)
-        take_larger(1)
-        gated(0, slice(0, J))
-        take_larger(2)
-        take_larger(3)
+        for t in (0, 2):
+            take_larger(t)
+            take_larger(t + 1)
+            gated(t, slice(0, J))
+            if t == 0:
+                gated(1, slice(0, J))
         for cols in halves:
-            gated(1, cols)
+            gated(3, cols)
+        for cols in halves:
+            nc.vector.tensor_copy(
+                out=hid[:, cols, :].rearrange("p (c i) t -> p c t i", i=4),
+                in_=hid_slots[:, :, cols].rearrange("p t (c i) -> p c t i", i=4),
+            )
 
         hid_w = sb.tile([P, J], U32, name="hid_w", align_bytes=64)
         hid_s = sb.tile([P, J], U8, name="hid_s", align_bytes=64)
-        p_bank = [ps.tile([P, J], F32, name=f"p_bank{h}", tag=f"left{h}") for h in range(2)]
+        p_bank = [ps.tile([P, 2, J // 2], F32, name=f"p_bank{c}", tag=f"left{c}") for c in range(2)]
         for cols in halves:
             nc.vector.quantize_mx(
                 out=hid_w[:, cols].bitcast(E5M2), scales=hid_s[:, cols], in_=hid[:, cols, :].rearrange("p j t -> p (j t)")
             )
-        for cols in halves:
+        for c, cols in enumerate(halves):
             for h in range(2):
                 nc.tensor.matmul_mx(
-                    out=p_bank[h][:, cols],
+                    out=p_bank[c][:, h, :],
                     lhsT=wb_w[:, 2 * h * P : 2 * (h + 1) * P].bitcast(E2M1),
                     lhsT_scale=wb_s[:, h * P : (h + 1) * P],
                     rhs=hid_w[:, cols].bitcast(E5M2),
@@ -201,9 +209,11 @@ def tile_list_crossed_tablegate_one_tabled_kernel(
                     stop=True,
                 )
 
+        picked = sb.tile([P, 2, J], F32, name="picked")
         for h in range(2):
-            picked = sb.tile([P, J], F32, name=f"picked{h}")
-            nc.scalar.activation(out=picked[:], in_=tz_rows[h][:].indirect(list_tz[:]), func=ACT.Copy)
-            result = sb.tile([P, J], F32, name=f"result{h}")
-            nc.vector.tensor_tensor(result[:], p_bank[h][:], picked[:], ALU.add)
-            nc.sync.dma_start(out=out[h * P : (h + 1) * P, :], in_=result[:])
+            nc.scalar.activation(out=picked[:, h, :], in_=tz_rows[h][:].indirect(list_tz[:]), func=ACT.Copy)
+        out_rows = out.rearrange("(h p) j -> p h j", p=P)
+        for c, cols in enumerate(halves):
+            result = sb.tile([P, 2, J // 2], F32, name=f"result{c}")
+            nc.vector.tensor_tensor(result[:], p_bank[c][:], picked[:, :, cols], ALU.add)
+            nc.sync.dma_start(out=out_rows[:, :, cols], in_=result[:])

@@ -70,12 +70,12 @@ def tile_list_crossed_tablegate_one_tabled_kernel(
         nc.sync.dma_start(out=xo_w[:].bitcast(I32), in_=xo_words[0].rearrange("p c r -> p (c r)").bitcast(I32))
         load_scale_rows(nc.sync, w_s, w_scales)
         nc.sync.dma_start(list_xo[:], offs2)
-        nc.sync.dma_start(out=w2_w[:].bitcast(I32), in_=w2_words[0].rearrange("p c r -> p (c r)").bitcast(I32))
-        nc.sync.dma_start(out=tg_rows[0][:], in_=tg_by_slot[0])
         nc.sync.dma_start(list_tg[:], offs3)
-        nc.sync.dma_start(out=tg_rows[1][:], in_=tg_by_slot[1])
+        nc.sync.dma_start(out=tg_rows[0][:], in_=tg_by_slot[0])
+        nc.sync.dma_start(out=w2_w[:].bitcast(I32), in_=w2_words[0].rearrange("p c r -> p (c r)").bitcast(I32))
         load_scale_rows(nc.sync, xo_s, xo_scales)
-        load_scale_rows(nc.sync, w2_s, w2_scales, (0, 1))
+        load_scale_rows(nc.sync, w2_s, w2_scales, (0,))
+        nc.sync.dma_start(out=tg_rows[1][:], in_=tg_by_slot[1])
         nc.sync.dma_start(out=tg_rows[2][:], in_=tg_by_slot[2])
         nc.sync.dma_start(list_tz[:], offs4)
         nc.sync.dma_start(out=tg_rows[3][:], in_=tg_by_slot[3])
@@ -86,7 +86,7 @@ def tile_list_crossed_tablegate_one_tabled_kernel(
 
         nc.gpsimd.dma_start(out=offset[:], in_=bg.rearrange("(p t) o -> p (t o)", t=PACK))
         nc.gpsimd.dma_start(out=slope[:], in_=sg.rearrange("(p t) o -> p (t o)", t=PACK))
-        load_scale_rows(nc.gpsimd, w2_s, w2_scales, (2, 3))
+        load_scale_rows(nc.gpsimd, w2_s, w2_scales, (1, 2, 3))
 
         xt_gw = sb.tile([P, J], U16, name="xt_gw", align_bytes=64)
         xt_gs = sb.tile([P, J], U8, name="xt_gs", align_bytes=64)
@@ -114,8 +114,8 @@ def tile_list_crossed_tablegate_one_tabled_kernel(
         deal_words(w_dw, w_w)
         deal_scales(w_ds, w_s)
         nc.vector.tensor_copy(xo_gw[:], xo_w[:].indirect(list_xo[:]))
-        nc.vector.tensor_copy(xo_gs[:], xo_s[:].indirect(list_xo[:]))
         deal_words(w2_dw, w2_w)
+        nc.vector.tensor_copy(xo_gs[:], xo_s[:].indirect(list_xo[:]))
         deal_scales(w2_ds, w2_s, slice(0, 2))
         deal_scales(w2_ds, w2_s, slice(2, PACK))
 
@@ -141,47 +141,50 @@ def tile_list_crossed_tablegate_one_tabled_kernel(
         for t in range(PACK):
             product(a_bank, t, first, tokens, True)
         for t in range(PACK):
-            product(b_bank, t, first, notes, True)
-        for t in range(PACK):
             product(a_bank, t, second, notes, False)
+            product(b_bank, t, first, notes, True)
             product(b_bank, t, second, tokens, False)
 
-        gate = sb.tile([P, PACK, J], F32, name="gate")
         hid = sb.tile([P, J, PACK], BF16, name="hid", align_bytes=64)
-        a_sb = sb.tile([P, PACK, J], F32, name="a_sb")
+        hid_slots = sb.tile([P, PACK, J], BF16, name="hid_slots")
         larger = sb.tile([P, PACK, J], F32, name="larger")
+        halves = [slice(0, J // 2), slice(J // 2, J)]
+        gate = {}
+        a_sb = {}
 
-        def look_up_gate(t):
+        def look_up_gate(t, tag):
+            gate[t] = sb.tile([P, J], F32, name=f"gate{t}", tag=tag)
             nc.scalar.activation(
-                out=gate[:, t, :], in_=tg_rows[t][:].indirect(list_tg[:]), func=ACT.Sigmoid,
+                out=gate[t][:], in_=tg_rows[t][:].indirect(list_tg[:]), func=ACT.Sigmoid,
                 bias=offset[:, t : t + 1], scale=slope[:, t : t + 1],
             )
 
+        def free_a(t):
+            a_sb[t] = sb.tile([P, J], F32, name=f"a_sb{t}", tag=f"a_copy{t}")
+            if t < 2:
+                nc.vector.tensor_copy(out=a_sb[t][:], in_=a_bank[t][:])
+            else:
+                nc.scalar.copy(out=a_sb[t][:], in_=a_bank[t][:])
+
         def take_larger(t):
-            nc.vector.tensor_tensor(larger[:, t, :], b_bank[t][:], a_sb[:, t, :], ALU.max)
+            nc.vector.tensor_tensor(larger[:, t, :], b_bank[t][:], a_sb[t][:], ALU.max)
 
         def gated(t, cols):
-            nc.vector.tensor_tensor(hid_slots[:, t, cols], larger[:, t, cols], gate[:, t, cols], ALU.mult)
+            nc.vector.tensor_tensor(hid_slots[:, t, cols], larger[:, t, cols], gate[t][:, cols], ALU.mult)
 
-        def free_a(t):
-            nc.scalar.copy(out=a_sb[:, t, :], in_=a_bank[t][:])
-
-        hid_slots = sb.tile([P, PACK, J], BF16, name="hid_slots")
-        halves = [slice(0, J // 2), slice(J // 2, J)]
-        look_up_gate(0)
-        look_up_gate(1)
-        free_a(0)
-        free_a(1)
-        look_up_gate(2)
-        free_a(2)
-        free_a(3)
-        look_up_gate(3)
-        for t in (0, 2):
+        for t in range(2):
+            look_up_gate(t, f"early_gate{t}")
+        for t in range(PACK):
+            free_a(t)
+        for t in range(2):
             take_larger(t)
-            take_larger(t + 1)
+        for t in range(2):
             gated(t, slice(0, J))
-            if t == 0:
-                gated(1, slice(0, J))
+        for t in range(2, PACK):
+            look_up_gate(t, f"a_copy{t - 2}")
+        for t in range(2, PACK):
+            take_larger(t)
+        gated(2, slice(0, J))
         for cols in halves:
             gated(3, cols)
         for cols in halves:
@@ -210,8 +213,10 @@ def tile_list_crossed_tablegate_one_tabled_kernel(
                 )
 
         picked = sb.tile([P, 2, J], F32, name="picked")
-        for h in range(2):
-            nc.scalar.activation(out=picked[:, h, :], in_=tz_rows[h][:].indirect(list_tz[:]), func=ACT.Copy)
+        nc.scalar.activation(out=picked[:, 0, :], in_=tz_rows[0][:].indirect(list_tz[:]), func=ACT.Copy)
+        for c, cols in enumerate(halves):
+            part = list_tz[:, c * (J // 32) : (c + 1) * (J // 32)]
+            nc.scalar.activation(out=picked[:, 1, cols], in_=tz_rows[1][:].indirect(part), func=ACT.Copy)
         out_rows = out.rearrange("(h p) j -> p h j", p=P)
         for c, cols in enumerate(halves):
             result = sb.tile([P, 2, J // 2], F32, name=f"result{c}")

from contextlib import ExitStack

import concourse.mybir as mybir

K, T, Z, J, R, Q, N, E = 512, 1024, 1024, 256, 512, 1024, 256, 1024
FLOPS = 2 * K * R * J * 4 + 2 * R * N * J

F32 = mybir.dt.float32
BF16 = mybir.dt.bfloat16
I32 = mybir.dt.int32
U32 = mybir.dt.uint32
U16 = mybir.dt.uint16
U8 = mybir.dt.uint8
E4M3 = mybir.dt.float8_e4m3fn_x4
E5M2 = mybir.dt.float8_e5m2_x4
E2M1 = mybir.dt.float4_e2m1fn_x4
ACT = mybir.ActivationFunctionType
ALU = mybir.AluOpType

P = 128
PACK = 4


def load_scale_rows(queue, plane, scales, quads=(0, 1, 2, 3)):
    rows = scales[0].bitcast(I32)
    for quad in quads:
        queue.dma_start(out=plane[32 * quad : 32 * quad + 4, :].bitcast(I32), in_=rows[4 * quad : 4 * quad + 4, :])


def tile_list_crossed_tablegate_one_tabled_kernel(
    tc, xt_words, xt_scales, xo_words, xo_scales, w_words, w_scales, w2_words, w2_scales,
    tg, sg, bg, wb_words, wb_scales, tz, offs, offs2, offs3, offs4, out,
):
    nc = tc.nc
    with ExitStack() as ctx:
        sb = ctx.enter_context(tc.tile_pool(name="sb", bufs=1))
        ps = ctx.enter_context(tc.psum_pool(name="ps", bufs=1))

        list_xt = sb.tile([P, J // 16], U16, name="list_xt")
        list_xo = sb.tile([P, J // 16], U16, name="list_xo")
        list_tg = sb.tile([P, J // 16], U16, name="list_tg")
        list_tz = sb.tile([P, J // 16], U16, name="list_tz")
        xt_w = sb.tile([P, T], U16, name="xt_w", align_bytes=64)
        xt_s = sb.tile([P, T], U8, name="xt_s", align_bytes=64)
        xo_w = sb.tile([P, Z], U32, name="xo_w", align_bytes=64)
        xo_s = sb.tile([P, Z], U8, name="xo_s", align_bytes=64)
        w_w = sb.tile([P, R], U32, name="w_w", align_bytes=64)
        w_s = sb.tile([P, R], U8, name="w_s", align_bytes=64)
        w2_w = sb.tile([P, R], U32, name="w2_w", align_bytes=64)
        w2_s = sb.tile([P, R], U8, name="w2_s", align_bytes=64)
        wb_w = sb.tile([P, 2 * N], U8, name="wb_w", align_bytes=64)
        wb_s = sb.tile([P, N], U8, name="wb_s", align_bytes=64)
        slope = sb.tile([P, PACK], F32, name="slope")
        offset = sb.tile([P, PACK], F32, name="offset")
        tg_rows = [sb.tile([P, Q], F32, name=f"tg_rows{t}") for t in range(PACK)]
        tz_rows = [sb.tile([P, E], F32, name=f"tz_rows{h}") for h in range(2)]

        nc.vector.memset(xt_s[:].bitcast(I32), 0)
        nc.vector.memset(w_s[:].bitcast(I32), 0)
        nc.vector.memset(xo_s[:].bitcast(I32), 0)
        nc.vector.memset(w2_s[:].bitcast(I32), 0)
        nc.vector.memset(wb_s[:].bitcast(I32), 0)

        tg_by_slot = tg.rearrange("(p t) q -> t p q", t=PACK)

        nc.sync.dma_start(out=xt_w[:].bitcast(I32), in_=xt_words[0].bitcast(I32))
        nc.sync.dma_start(list_xt[:], offs)
        load_scale_rows(nc.sync, xt_s, xt_scales)
        nc.sync.dma_start(out=w_w[:].bitcast(I32), in_=w_words[0].rearrange("p c r -> p (c r)").bitcast(I32))
        nc.sync.dma_start(out=xo_w[:].bitcast(I32), in_=xo_words[0].rearrange("p c r -> p (c r)").bitcast(I32))
        load_scale_rows(nc.sync, w_s, w_scales)
        nc.sync.dma_start(list_xo[:], offs2)
        nc.sync.dma_start(list_tg[:], offs3)
        nc.sync.dma_start(out=tg_rows[0][:], in_=tg_by_slot[0])
        nc.sync.dma_start(out=w2_w[:].bitcast(I32), in_=w2_words[0].rearrange("p c r -> p (c r)").bitcast(I32))
        load_scale_rows(nc.sync, xo_s, xo_scales)
        load_scale_rows(nc.sync, w2_s, w2_scales, (0,))
        nc.sync.dma_start(out=tg_rows[1][:], in_=tg_by_slot[1])
        nc.sync.dma_start(out=tg_rows[2][:], in_=tg_by_slot[2])
        nc.sync.dma_start(list_tz[:], offs4)
        nc.sync.dma_start(out=tg_rows[3][:], in_=tg_by_slot[3])
        nc.sync.dma_start(out=tz_rows[0][:], in_=tz[0:P, :])
        nc.sync.dma_start(out=wb_w[:].bitcast(I32), in_=wb_words[0].bitcast(I32))
        load_scale_rows(nc.sync, wb_s, wb_scales)
        nc.sync.dma_start(out=tz_rows[1][:], in_=tz[P : 2 * P, :])

        nc.gpsimd.dma_start(out=offset[:], in_=bg.rearrange("(p t) o -> p (t o)", t=PACK))
        nc.gpsimd.dma_start(out=slope[:], in_=sg.rearrange("(p t) o -> p (t o)", t=PACK))
        load_scale_rows(nc.gpsimd, w2_s, w2_scales, (1, 2, 3))

        xt_gw = sb.tile([P, J], U16, name="xt_gw", align_bytes=64)
        xt_gs = sb.tile([P, J], U8, name="xt_gs", align_bytes=64)
        xo_gw = sb.tile([P, J], U32, name="xo_gw", align_bytes=64)
        xo_gs = sb.tile([P, J], U8, name="xo_gs", align_bytes=64)
        w_dw = sb.tile([P, R], U32, name="w_dw", align_bytes=64)
        w_ds = sb.tile([P, R], U8, name="w_ds", align_bytes=64)
        w2_dw = sb.tile([P, R], U32, name="w2_dw", align_bytes=64)
        w2_ds = sb.tile([P, R], U8, name="w2_ds", align_bytes=64)

        def deal_words(dst, src):
            nc.vector.tensor_copy(
                out=dst[:].bitcast(I32).rearrange("p (t c i) -> p c t i", t=PACK, i=4),
                in_=src[:].bitcast(I32).rearrange("p (c i t) -> p c t i", t=PACK, i=4),
            )

        def deal_scales(dst, src, slots=slice(0, PACK)):
            nc.vector.tensor_copy(
                out=dst[:].rearrange("p (t m) -> p t m", t=PACK)[:, slots, :],
                in_=src[:].rearrange("p (m t) -> p t m", t=PACK)[:, slots, :],
            )

        nc.vector.tensor_copy(xt_gw[:], xt_w[:].indirect(list_xt[:]))
        nc.vector.tensor_copy(xt_gs[:], xt_s[:].indirect(list_xt[:]))
        deal_words(w_dw, w_w)
        deal_scales(w_ds, w_s)
        nc.vector.tensor_copy(xo_gw[:], xo_w[:].indirect(list_xo[:]))
        deal_words(w2_dw, w2_w)
        nc.vector.tensor_copy(xo_gs[:], xo_s[:].indirect(list_xo[:]))
        deal_scales(w2_ds, w2_s, slice(0, 2))
        deal_scales(w2_ds, w2_s, slice(2, PACK))

        a_bank = [ps.tile([P, J], F32, name=f"a_bank{t}", tag=f"left{t}") for t in range(PACK)]
        b_bank = [ps.tile([P, J], F32, name=f"b_bank{t}", tag=f"right{t}") for t in range(PACK)]
        first = (w_dw, w_ds, E4M3)
        second = (w2_dw, w2_ds, E5M2)
        tokens = (xt_gw, xt_gs, E2M1)
        notes = (xo_gw, xo_gs, E4M3)

        def product(bank, t, weight, moving, opens):
            cols = slice(t * P, (t + 1) * P)
            nc.tensor.matmul_mx(
                out=bank[t][:],
                lhsT=weight[0][:, cols].bitcast(weight[2]),
                lhsT_scale=weight[1][:, cols],
                rhs=moving[0][:].bitcast(moving[2]),
                rhs_scale=moving[1][:],
                start=opens,
                stop=not opens,
            )

        for t in range(PACK):
            product(a_bank, t, first, tokens, True)
        for t in range(PACK):
            product(a_bank, t, second, notes, False)
            product(b_bank, t, first, notes, True)
            product(b_bank, t, second, tokens, False)

        hid = sb.tile([P, J, PACK], BF16, name="hid", align_bytes=64)
        hid_slots = sb.tile([P, PACK, J], BF16, name="hid_slots")
        larger = sb.tile([P, PACK, J], F32, name="larger")
        halves = [slice(0, J // 2), slice(J // 2, J)]
        gate = {}
        a_sb = {}

        def look_up_gate(t, tag):
            gate[t] = sb.tile([P, J], F32, name=f"gate{t}", tag=tag)
            nc.scalar.activation(
                out=gate[t][:], in_=tg_rows[t][:].indirect(list_tg[:]), func=ACT.Sigmoid,
                bias=offset[:, t : t + 1], scale=slope[:, t : t + 1],
            )

        def free_a(t):
            a_sb[t] = sb.tile([P, J], F32, name=f"a_sb{t}", tag=f"a_copy{t}")
            if t < 2:
                nc.vector.tensor_copy(out=a_sb[t][:], in_=a_bank[t][:])
            else:
                nc.scalar.copy(out=a_sb[t][:], in_=a_bank[t][:])

        def take_larger(t):
            nc.vector.tensor_tensor(larger[:, t, :], b_bank[t][:], a_sb[t][:], ALU.max)

        def gated(t, cols):
            nc.vector.tensor_tensor(hid_slots[:, t, cols], larger[:, t, cols], gate[t][:, cols], ALU.mult)

        for t in range(2):
            look_up_gate(t, f"early_gate{t}")
        for t in range(PACK):
            free_a(t)
        for t in range(2):
            take_larger(t)
        for t in range(2):
            gated(t, slice(0, J))
        for t in range(2, PACK):
            look_up_gate(t, f"a_copy{t - 2}")
        for t in range(2, PACK):
            take_larger(t)
        gated(2, slice(0, J))
        for cols in halves:
            gated(3, cols)
        for cols in halves:
            nc.vector.tensor_copy(
                out=hid[:, cols, :].rearrange("p (c i) t -> p c t i", i=4),
                in_=hid_slots[:, :, cols].rearrange("p t (c i) -> p c t i", i=4),
            )

        hid_w = sb.tile([P, J], U32, name="hid_w", align_bytes=64)
        hid_s = sb.tile([P, J], U8, name="hid_s", align_bytes=64)
        p_bank = [ps.tile([P, 2, J // 2], F32, name=f"p_bank{c}", tag=f"left{c}") for c in range(2)]
        for cols in halves:
            nc.vector.quantize_mx(
                out=hid_w[:, cols].bitcast(E5M2), scales=hid_s[:, cols], in_=hid[:, cols, :].rearrange("p j t -> p (j t)")
            )
        for c, cols in enumerate(halves):
            for h in range(2):
                nc.tensor.matmul_mx(
                    out=p_bank[c][:, h, :],
                    lhsT=wb_w[:, 2 * h * P : 2 * (h + 1) * P].bitcast(E2M1),
                    lhsT_scale=wb_s[:, h * P : (h + 1) * P],
                    rhs=hid_w[:, cols].bitcast(E5M2),
                    rhs_scale=hid_s[:, cols],
                    start=True,
                    stop=True,
                )

        picked = sb.tile([P, 2, J], F32, name="picked")
        nc.scalar.activation(out=picked[:, 0, :], in_=tz_rows[0][:].indirect(list_tz[:]), func=ACT.Copy)
        for c, cols in enumerate(halves):
            part = list_tz[:, c * (J // 32) : (c + 1) * (J // 32)]
            nc.scalar.activation(out=picked[:, 1, cols], in_=tz_rows[1][:].indirect(part), func=ACT.Copy)
        out_rows = out.rearrange("(h p) j -> p h j", p=P)
        for c, cols in enumerate(halves):
            result = sb.tile([P, 2, J // 2], F32, name=f"result{c}")
            nc.vector.tensor_tensor(result[:], p_bank[c][:], picked[:, :, cols], ALU.add)
            nc.sync.dma_start(out=out_rows[:, :, cols], in_=result[:])
